import numpy as np
import ml_dtypes


def mxq(x, axis, fmt="e4m3"):
    dtype, down = {"e4m3": (ml_dtypes.float8_e4m3fn, 7), "e5m2": (ml_dtypes.float8_e5m2, 14)}[fmt]
    v = np.moveaxis(np.asarray(x, np.float32).astype(ml_dtypes.bfloat16).astype(np.float64), axis, -1)
    blocks = v.reshape(v.shape[:-1] + (-1, 32))
    amax = np.abs(blocks).max(-1, keepdims=True)
    byte = np.maximum(np.where(amax > 0, np.frexp(amax)[1] - 1 + 127, 0) - down, 1)
    scale = np.exp2(byte - 127.0)
    codes = (blocks / scale).astype(np.float32).astype(dtype).astype(np.float64)
    return np.moveaxis((codes * scale).reshape(v.shape), -1, axis)


WIDE = False


def mx_kscale(k):
    if not WIDE:
        return np.ones(k)
    levels = np.array([10, -10, 5, -5, 0])
    if k % 512:
        return np.exp2(np.random.permutation(np.resize(levels, k // 32))).repeat(32)
    a = np.empty((k // 512, 16))
    for p in range(k // 512):
        a[p, :8] = np.random.permutation(np.resize(levels, 8))
        for g in range(8):
            far = levels[np.abs(levels - a[p, g]) >= 10]
            a[p, g + 8] = far[np.random.randint(len(far))]
    return np.exp2(a.ravel()).repeat(32)


def f64(x):
    return np.asarray(x).astype(np.float64)


def striped(idx):
    return np.tile(np.asarray(idx).reshape(-1, 16).T, (8, 1)).astype(np.uint16)


def unstriped(offs):
    return offs[:16].T.reshape(-1).astype(np.int64)


E2M1 = np.array([0.0, 0.5, 1.0, 1.5, 2.0, 3.0, 4.0, 6.0, -0.0, -0.5, -1.0, -1.5, -2.0, -3.0, -4.0, -6.0])


def pack_weight(w, fmt):
    k, n = w.shape
    w = f64(np.asarray(w, np.float32).astype(ml_dtypes.bfloat16)).reshape(k // 32, 32, n)
    amax = np.abs(w).max(1)
    if fmt == "e4m3":
        byte = np.frexp(amax)[1] - 1 + 127 - 7
    else:
        mant, ex = np.frexp(amax / 6.0)
        byte = np.where(mant > 0.5, ex, ex - 1) + 127
    byte = np.clip(np.where(amax > 0, byte, 1), 1, 254)
    scaled = (w * np.exp2(127.0 - byte)[:, None, :]).reshape(k, n).astype(np.float32)
    by_word = np.ascontiguousarray(scaled.reshape(k // 512, 128, 4, n).transpose(0, 1, 3, 2))
    if fmt == "e4m3":
        words = by_word.astype(ml_dtypes.float8_e4m3fn).view(np.uint8)
    else:
        c = by_word.astype(ml_dtypes.float4_e2m1fn).view(np.uint8) & 0xF
        words = (c[..., 0::2] | (c[..., 1::2] << 4)).reshape(k // 512, 128, 2 * n)
    return np.ascontiguousarray(words), np.ascontiguousarray(byte.astype(np.uint8).reshape(k // 512, 16, n))


def unpack_weight(words, scales, fmt):
    g, _, n = scales.shape
    words = np.ascontiguousarray(words).reshape(g, 128, n, -1)
    if fmt == "e4m3":
        vals = words.view(ml_dtypes.float8_e4m3fn).astype(np.float64)
    else:
        nib = np.empty((g, 128, n, 4), np.uint8)
        nib[..., 0::2] = words & 0xF
        nib[..., 1::2] = words >> 4
        vals = E2M1[nib]
    vals = vals * np.repeat(np.exp2(scales.astype(np.float64) - 127.0), 8, axis=1)[..., None]
    return vals.transpose(0, 1, 3, 2).reshape(g * 512, n)


def sigmoid(v):
    return 1.0 / (1.0 + np.exp(-v))


D, K, R, T, I, Q, U = 512, 512, 512, 2048, 512, 128, 1024


def setup_inputs():
    n = np.random.standard_normal
    idx2 = np.random.permutation(U)[:I]
    idx = np.random.permutation(T)[:I]
    fd = mx_kscale(D)
    fk = mx_kscale(K)
    fr = mx_kscale(R)
    keysp = pack_weight(n((D, T)) / fd[:, None], "e4m3")
    tabp = pack_weight(n((K, T)) / fk[:, None], "e4m3")
    return {
        "query": (n((D, Q)) * 0.6 / np.sqrt(D) * fd[:, None]).astype(np.float32),
        "query2": (n((D, Q)) * 1.0 / np.sqrt(D) * fd[:, None]).astype(np.float32),
        "keys_words": keysp[0],
        "keys_scales": keysp[1],
        "tab_words": tabp[0],
        "tab_scales": tabp[1],
        "w1": (n((K, R)) * 1 / np.sqrt(K) * fk[:, None]).astype(np.float32),
        "gtab": (n((R, U))).astype(np.float32),
        "gout": (n((R, Q)) * 1 / np.sqrt(R) * fr[:, None]).astype(np.float32),
        "hsc": (np.random.uniform(0.7, 1.4, (R, 1)) / fr[:, None]).astype(np.float32),
        "old": (0.5 * n((Q, T))).astype(np.float32),
        "offs2": striped(idx2),
        "offs": striped(idx),
    }


def reference(query, query2, keys_words, keys_scales, tab_words, tab_scales, w1, gtab, gout, hsc, old, offs2, offs):
    idx2 = unstriped(offs2)
    idx = unstriped(offs)
    keysu = unpack_weight(keys_words, keys_scales, "e4m3")
    tabu = unpack_weight(tab_words, tab_scales, "e4m3")
    queryq = mxq(f64(query), 0, "e4m3")
    keysidxg = keysu[:, idx]
    a = queryq.T @ keysidxg
    query2q = mxq(f64(query2), 0, "e4m3")
    b = query2q.T @ keysidxg
    p = np.exp(a - np.max(a, axis=1, keepdims=True)) * sigmoid(b)
    z = np.sum(p, axis=1, keepdims=True)
    w1q = mxq(f64(w1), 0, "e4m3")
    tabidxg = tabu[:, idx]
    zh = w1q.T @ tabidxg
    hg = sigmoid(f64(gtab)[:, idx2])
    hv = zh * hg
    hs1 = hv * f64(hsc)
    goutq = mxq(f64(gout), 0, "e4m3")
    hs1q = mxq(hs1, 0, "e4m3")
    c0 = goutq.T @ hs1q
    dz = np.sum(c0 * p / np.square(z) * (-1.0), axis=1, keepdims=True)
    dp = c0 / z + dz
    da = dp * sigmoid(b) * np.exp(a - np.max(a, axis=1, keepdims=True))
    gs = da * 512.0
    gf = np.zeros((Q, T))
    gf[:, idx] = gs
    y = f64(old) + gf
    return y

@@ -1,0 +1,201 @@
+from contextlib import ExitStack
+
+import concourse.mybir as mybir
+
+D, K, R, T, I, Q, U = 512, 512, 512, 2048, 512, 128, 1024
+FLOPS = 2 * D * Q * I * 2 + 2 * K * R * I + 2 * R * Q * I
+
+F32 = mybir.dt.float32
+BF16 = mybir.dt.bfloat16
+I32 = mybir.dt.int32
+U32 = mybir.dt.uint32
+U16 = mybir.dt.uint16
+U8 = mybir.dt.uint8
+FP8X4 = mybir.dt.float8_e4m3fn_x4
+ALU = mybir.AluOpType
+ACT = mybir.ActivationFunctionType
+AXIS = mybir.AxisListType
+
+P = 128
+PACK = 4
+HALF = I // 2
+TAB_PLANE = 4
+SCALAR_SLOTS = 96
+OUT_EDGES = (0, 256, 768, 1280, 1792, 2048)
+
+
+def tile_attend_blrgated_asked_kernel(
+    tc, query, query2, keys_words, keys_scales, tab_words, tab_scales, w1, gtab, gout, hsc, old, offs2, offs, out
+):
+    nc = tc.nc
+    with ExitStack() as ctx:
+        sb = ctx.enter_context(tc.tile_pool(name="sb", bufs=1))
+        ps = ctx.enter_context(tc.psum_pool(name="ps", bufs=1))
+
+        def tile(name, shape, dtype, tag=None):
+            return sb.tile(shape, dtype, name=name, tag=tag or name, align_bytes=64)
+
+        def bank(name):
+            return ps.tile([P, I], F32, name=name)
+
+        def load_rows(name, src):
+            raw = tile(name, [P, PACK, src.shape[1]], F32)
+            nc.sync.dma_start(out=raw[:], in_=src.rearrange("(p j) w -> p j w", j=PACK))
+            return raw
+
+        def load_words(name, src):
+            pool_words = tile(name, [P, T], I32)
+            nc.sync.dma_start(out=pool_words[:], in_=src[0].rearrange("p n t -> p (n t)").bitcast(I32))
+            return pool_words
+
+        def load_scales(queue, plane, src, first):
+            rows = src[0].rearrange("(g r) c -> r g c", r=PACK)
+            for r in range(PACK):
+                queue.dma_start(out=plane[first + r : P : 32, :].bitcast(I32), in_=rows[r].bitcast(I32))
+
+        def quantise(name, grouped, width):
+            codes = tile(name + "_codes", [P, width], U32)
+            scales = tile(name + "_scales", [P, width], U8)
+            nc.vector.quantize_mx(out=codes[:].bitcast(FP8X4), scales=scales[:], in_=grouped)
+            return codes, scales
+
+        def interleave_on_scalar(name, raw):
+            grouped = tile(name, [P, Q, PACK], BF16)
+            nc.scalar.copy(out=grouped[:], in_=raw[:].rearrange("p j w -> p w j"))
+            return grouped[:].rearrange("p w j -> p (w j)")
+
+        def product(acc, lhs, lhs_scale, rhs, rhs_scale):
+            nc.tensor.matmul_mx(
+                out=acc, lhsT=lhs.bitcast(FP8X4), lhsT_scale=lhs_scale,
+                rhs=rhs.bitcast(FP8X4), rhs_scale=rhs_scale, start=True, stop=True,
+            )
+
+        key_plane = tile("key_plane", [P, T], U8)
+        tab_plane = tile("tab_plane", [P, T], U8)
+        spread = tile("spread", [P, T], F32)
+        nc.vector.memset(key_plane[:].bitcast(I32), 0)
+        nc.vector.memset(tab_plane[:].bitcast(I32), 0)
+        nc.vector.memset(spread[:], 0.0)
+
+        tokens = tile("tokens", [P, I // 16], U16)
+        gates = tile("gates", [P, I // 16], U16)
+        nc.sync.dma_start(out=tokens[:], in_=offs)
+        q_raw = load_rows("q_raw", query)
+        load_scales(nc.scalar, key_plane, keys_scales, 0)
+        key_pool = load_words("key_pool", keys_words)
+        q_grouped = interleave_on_scalar("q_grouped", q_raw)
+        load_scales(nc.scalar, tab_plane, tab_scales, TAB_PLANE)
+        q2_raw = load_rows("q2_raw", query2)
+        w_raw = load_rows("w_raw", w1)
+        nc.sync.dma_start(out=gates[:], in_=offs2)
+        hsc_sb = tile("hsc_sb", [P, PACK], F32)
+        gate_rows = gtab.rearrange("(p j) u -> j p u", j=PACK)
+        gate_pool = []
+        for j in range(PACK):
+            gate_pool.append(tile("gate_pool%d" % j, [P, U], F32))
+            nc.sync.dma_start(out=gate_pool[j][:], in_=gate_rows[j])
+            if j == 0:
+                tab_pool = load_words("tab_pool", tab_words)
+            if j == 1:
+                nc.sync.dma_start(out=hsc_sb[:], in_=hsc.rearrange("(p j) o -> p (j o)", j=PACK))
+        gout_raw = load_rows("gout_raw", gout)
+        old_sb = tile("old_sb", [P, T], F32)
+        nc.sync.dma_start(out=old_sb[:], in_=old)
+
+        key_scales = tile("key_scales", [P, I], U8)
+        nc.vector.tensor_copy(out=key_scales[:], in_=key_plane[:].indirect(tokens[:]))
+        q_codes, q_scales = quantise("q", q_grouped, Q)
+        key_codes = tile("key_codes", [P, I], U32)
+        nc.vector.tensor_copy(out=key_codes[:], in_=key_pool[:].bitcast(U32).indirect(tokens[:]))
+        score = bank("score")
+        product(score[:], q_codes[:], q_scales[:], key_codes[:], key_scales[:])
+        q2_codes, q2_scales = quantise("q2", interleave_on_scalar("q2_grouped", q2_raw), Q)
+        score2 = bank("score2")
+        product(score2[:], q2_codes[:], q2_scales[:], key_codes[:], key_scales[:])
+        neg_max = tile("neg_max", [P, 1], F32)
+        nc.vector.tensor_reduce(out=neg_max[:], in_=score[:], axis=AXIS.X, op=ALU.max, negate=True)
+        expd = tile("expd", [P, I], F32)
+        nc.scalar.activation(out=expd[:], in_=score[:], func=ACT.Exp, bias=neg_max[:])
+        sig2 = tile("sig2", [P, I], F32)
+        nc.scalar.activation(out=sig2[:], in_=score2[:], func=ACT.Sigmoid)
+
+        tab_sc = tile("tab_sc", [P, I], U8)
+        nc.vector.tensor_copy(out=tab_sc[:], in_=tab_plane[:].indirect(tokens[:]))
+        w_grouped = tile("w_grouped", [P, PACK, P, PACK], BF16)
+        nc.vector.tensor_copy(
+            out=w_grouped[:].rearrange("p t m j -> p m t j"),
+            in_=w_raw[:].rearrange("p j (m t) -> p m t j", t=PACK),
+        )
+        w_codes, w_scales = quantise("w", w_grouped[:].rearrange("p t m j -> p (t m j)"), R)
+        tab_codes = tile("tab_codes", [P, I], U32)
+        nc.vector.tensor_copy(out=tab_codes[:], in_=tab_pool[:].bitcast(U32).indirect(tokens[:]))
+        hidden = []
+        for t in range(PACK):
+            hidden.append(bank("hidden%d" % t))
+            cols = slice(t * P, (t + 1) * P)
+            product(hidden[t][:], w_codes[:, cols], w_scales[:, cols], tab_codes[:], tab_sc[TAB_PLANE:P, :])
+
+        weights = tile("weights", [P, I], F32, tag="tab_pool")
+        total = tile("total", [P, 1], F32)
+        nc.vector.scalar_tensor_tensor(
+            out=weights[:], in0=expd[:], scalar=1.0, in1=sig2[:], op0=ALU.mult, op1=ALU.mult, accum_out=total[:]
+        )
+        inv_total = tile("inv_total", [P, 1], F32)
+        nc.vector.reciprocal(out=inv_total[:], in_=total[:])
+        up = tile("up", [P, 1], F32)
+        nc.vector.tensor_scalar(out=up[:], in0=inv_total[:], scalar1=512.0, scalar2=None, op0=ALU.mult)
+        down = tile("down", [P, 1], F32)
+        nc.vector.tensor_scalar(out=down[:], in0=inv_total[:], scalar1=-1.0, scalar2=None, op0=ALU.mult)
+
+        halves = [slice(0, HALF), slice(HALF, I)]
+        planes = [tile("planes%d" % h, [P, PACK, HALF], BF16) for h in range(2)]
+        for t in range(PACK):
+            if t < PACK - 1:
+                gate = tile("gate%d" % t, [P, I], F32)
+                nc.scalar.activation(out=gate[:], in_=gate_pool[t][:].indirect(gates[:]), func=ACT.Sigmoid)
+                pieces = [gate[:, halves[0]], gate[:, halves[1]]]
+            else:
+                pieces = []
+                for h in range(2):
+                    gate = tile("gate_last%d" % h, [P, HALF], F32)
+                    nc.scalar.activation(
+                        out=gate[:], in_=gate_pool[t][:].indirect(gates[:, h * 16 : (h + 1) * 16]), func=ACT.Sigmoid
+                    )
+                    pieces.append(gate[:])
+            for h in range(2):
+                nc.vector.scalar_tensor_tensor(
+                    out=planes[h][:, t, :], in0=hidden[t][:, halves[h]], scalar=hsc_sb[:, t : t + 1], in1=pieces[h],
+                    op0=ALU.mult, op1=ALU.mult,
+                )
+        gout_codes, gout_scales = quantise("gout", interleave_on_scalar("gout_grouped", gout_raw), Q)
+
+        grad = bank("grad")
+        for h in range(2):
+            grouped = tile("hs_grouped%d" % h, [P, HALF, PACK], BF16)
+            src = planes[h][:].rearrange("p t i -> p i t")
+            if h == 0:
+                nc.vector.tensor_copy(out=grouped[:], in_=src)
+            else:
+                nc.scalar.copy(out=grouped[:, :SCALAR_SLOTS, :], in_=src[:, :SCALAR_SLOTS, :])
+                nc.vector.tensor_copy(out=grouped[:, SCALAR_SLOTS:, :], in_=src[:, SCALAR_SLOTS:, :])
+            hs_codes, hs_scales = quantise("hs%d" % h, grouped[:].rearrange("p i t -> p (i t)"), HALF)
+            product(grad[:, halves[h]], gout_codes[:], gout_scales[:], hs_codes[:], hs_scales[:])
+
+        direct = tile("direct", [P, I], F32)
+        direct_sum = tile("direct_sum", [P, 1], F32)
+        nc.vector.scalar_tensor_tensor(
+            out=direct[:], in0=grad[:], scalar=up[:], in1=weights[:], op0=ALU.mult, op1=ALU.mult,
+            accum_out=direct_sum[:],
+        )
+        through_sum = tile("through_sum", [P, I], F32)
+        nc.vector.tensor_scalar(
+            out=through_sum[:], in0=weights[:], scalar1=direct_sum[:], scalar2=down[:], op0=ALU.mult, op1=ALU.mult
+        )
+        nc.vector.tensor_tensor(out=spread[:].indirect(tokens[:]), in0=direct[:], in1=through_sum[:], op=ALU.add)
+
+        for c in range(len(OUT_EDGES) - 1):
+            cols = slice(OUT_EDGES[c], OUT_EDGES[c + 1])
+            result = tile("result%d" % c, [P, cols.stop - cols.start], F32)
+            nc.vector.tensor_tensor(out=result[:], in0=spread[:, cols], in1=old_sb[:, cols], op=ALU.add)
+            queue = nc.sync if c % 2 == 0 else nc.scalar
+            queue.dma_start(out=out[:, cols], in_=result[:])

@@ -20,7 +20,7 @@ P = 128
 PACK = 4
 HALF = I // 2
 TAB_PLANE = 4
-SCALAR_SLOTS = 96
+SCALAR_SLOTS = 128
 OUT_EDGES = (0, 256, 768, 1280, 1792, 2048)
 
 
@@ -35,8 +35,8 @@ def tile_attend_blrgated_asked_kernel(
         def tile(name, shape, dtype, tag=None):
             return sb.tile(shape, dtype, name=name, tag=tag or name, align_bytes=64)
 
-        def bank(name):
-            return ps.tile([P, I], F32, name=name)
+        def bank(name, width=I):
+            return ps.tile([P, width], F32, name=name)
 
         def load_rows(name, src):
             raw = tile(name, [P, PACK, src.shape[1]], F32)
@@ -61,7 +61,10 @@ def tile_attend_blrgated_asked_kernel(
 
         def interleave_on_scalar(name, raw):
             grouped = tile(name, [P, Q, PACK], BF16)
-            nc.scalar.copy(out=grouped[:], in_=raw[:].rearrange("p j w -> p w j"))
+            nc.scalar.copy(
+                out=grouped[:].rearrange("p (c i) j -> p c j i", i=PACK),
+                in_=raw[:].rearrange("p j (c i) -> p c j i", i=PACK),
+            )
             return grouped[:].rearrange("p w j -> p (w j)")
 
         def product(acc, lhs, lhs_scale, rhs, rhs_scale):
@@ -81,11 +84,11 @@ def tile_attend_blrgated_asked_kernel(
         gates = tile("gates", [P, I // 16], U16)
         nc.sync.dma_start(out=tokens[:], in_=offs)
         q_raw = load_rows("q_raw", query)
-        load_scales(nc.scalar, key_plane, keys_scales, 0)
+        q2_raw = load_rows("q2_raw", query2)
+        load_scales(nc.sync, key_plane, keys_scales, 0)
         key_pool = load_words("key_pool", keys_words)
         q_grouped = interleave_on_scalar("q_grouped", q_raw)
-        load_scales(nc.scalar, tab_plane, tab_scales, TAB_PLANE)
-        q2_raw = load_rows("q2_raw", query2)
+        load_scales(nc.sync, tab_plane, tab_scales, TAB_PLANE)
         w_raw = load_rows("w_raw", w1)
         nc.sync.dma_start(out=gates[:], in_=offs2)
         hsc_sb = tile("hsc_sb", [P, PACK], F32)
@@ -105,26 +108,37 @@ def tile_attend_blrgated_asked_kernel(
         key_scales = tile("key_scales", [P, I], U8)
         nc.vector.tensor_copy(out=key_scales[:], in_=key_plane[:].indirect(tokens[:]))
         q_codes, q_scales = quantise("q", q_grouped, Q)
-        key_codes = tile("key_codes", [P, I], U32)
-        nc.vector.tensor_copy(out=key_codes[:], in_=key_pool[:].bitcast(U32).indirect(tokens[:]))
-        score = bank("score")
-        product(score[:], q_codes[:], q_scales[:], key_codes[:], key_scales[:])
+        halves = [slice(0, HALF), slice(HALF, I)]
         q2_codes, q2_scales = quantise("q2", interleave_on_scalar("q2_grouped", q2_raw), Q)
+        key_codes = tile("key_codes", [P, I], U32)
+        score = [bank("score%d" % h, HALF) for h in range(2)]
+        for h in range(2):
+            nc.vector.tensor_copy(
+                out=key_codes[:, halves[h]], in_=key_pool[:].bitcast(U32).indirect(tokens[:, h * 16 : (h + 1) * 16])
+            )
+            product(score[h][:], q_codes[:], q_scales[:], key_codes[:, halves[h]], key_scales[:, halves[h]])
         score2 = bank("score2")
         product(score2[:], q2_codes[:], q2_scales[:], key_codes[:], key_scales[:])
+        neg_max_first = tile("neg_max_first", [P, 1], F32)
+        nc.vector.tensor_reduce(out=neg_max_first[:], in_=score[0][:], axis=AXIS.X, op=ALU.max, negate=True)
         neg_max = tile("neg_max", [P, 1], F32)
-        nc.vector.tensor_reduce(out=neg_max[:], in_=score[:], axis=AXIS.X, op=ALU.max, negate=True)
+        neg_score = tile("neg_score", [P, HALF], F32)
+        nc.vector.tensor_scalar(
+            out=neg_score[:], in0=score[1][:], scalar1=-1.0, scalar2=neg_max_first[:], op0=ALU.mult, op1=ALU.min,
+            accum_out=neg_max[:],
+        )
         expd = tile("expd", [P, I], F32)
-        nc.scalar.activation(out=expd[:], in_=score[:], func=ACT.Exp, bias=neg_max[:])
-        sig2 = tile("sig2", [P, I], F32)
+        nc.scalar.activation(out=expd[:, halves[0]], in_=score[0][:], func=ACT.Exp, bias=neg_max[:])
+        nc.scalar.activation(out=expd[:, halves[1]], in_=neg_score[:], func=ACT.Exp, bias=neg_max[:], scale=-1.0)
+        sig2 = tile("sig2", [P, I], F32, tag="neg_score")
         nc.scalar.activation(out=sig2[:], in_=score2[:], func=ACT.Sigmoid)
 
         tab_sc = tile("tab_sc", [P, I], U8)
         nc.vector.tensor_copy(out=tab_sc[:], in_=tab_plane[:].indirect(tokens[:]))
         w_grouped = tile("w_grouped", [P, PACK, P, PACK], BF16)
         nc.vector.tensor_copy(
-            out=w_grouped[:].rearrange("p t m j -> p m t j"),
-            in_=w_raw[:].rearrange("p j (m t) -> p m t j", t=PACK),
+            out=w_grouped[:].rearrange("p t m j -> p m j t"),
+            in_=w_raw[:].rearrange("p j (m t) -> p m j t", t=PACK),
         )
         w_codes, w_scales = quantise("w", w_grouped[:].rearrange("p t m j -> p (t m j)"), R)
         tab_codes = tile("tab_codes", [P, I], U32)
@@ -147,13 +161,12 @@ def tile_attend_blrgated_asked_kernel(
         down = tile("down", [P, 1], F32)
         nc.vector.tensor_scalar(out=down[:], in0=inv_total[:], scalar1=-1.0, scalar2=None, op0=ALU.mult)
 
-        halves = [slice(0, HALF), slice(HALF, I)]
-        planes = [tile("planes%d" % h, [P, PACK, HALF], BF16) for h in range(2)]
+        planes = tile("planes", [P, PACK, I], BF16)
         for t in range(PACK):
             if t < PACK - 1:
                 gate = tile("gate%d" % t, [P, I], F32)
                 nc.scalar.activation(out=gate[:], in_=gate_pool[t][:].indirect(gates[:]), func=ACT.Sigmoid)
-                pieces = [gate[:, halves[0]], gate[:, halves[1]]]
+                pieces = [(slice(0, I), gate[:])]
             else:
                 pieces = []
                 for h in range(2):
@@ -161,10 +174,10 @@ def tile_attend_blrgated_asked_kernel(
                     nc.scalar.activation(
                         out=gate[:], in_=gate_pool[t][:].indirect(gates[:, h * 16 : (h + 1) * 16]), func=ACT.Sigmoid
                     )
-                    pieces.append(gate[:])
-            for h in range(2):
+                    pieces.append((halves[h], gate[:]))
+            for slots, piece in pieces:
                 nc.vector.scalar_tensor_tensor(
-                    out=planes[h][:, t, :], in0=hidden[t][:, halves[h]], scalar=hsc_sb[:, t : t + 1], in1=pieces[h],
+                    out=planes[:, t, slots], in0=hidden[t][:, slots], scalar=hsc_sb[:, t : t + 1], in1=piece,
                     op0=ALU.mult, op1=ALU.mult,
                 )
         gout_codes, gout_scales = quantise("gout", interleave_on_scalar("gout_grouped", gout_raw), Q)
@@ -172,12 +185,14 @@ def tile_attend_blrgated_asked_kernel(
         grad = bank("grad")
         for h in range(2):
             grouped = tile("hs_grouped%d" % h, [P, HALF, PACK], BF16)
-            src = planes[h][:].rearrange("p t i -> p i t")
+            src = planes[:, :, halves[h]].rearrange("p t (c i) -> p c t i", i=PACK)
+            dst = grouped[:].rearrange("p (c i) t -> p c t i", i=PACK)
             if h == 0:
-                nc.vector.tensor_copy(out=grouped[:], in_=src)
+                nc.vector.tensor_copy(out=dst, in_=src)
             else:
-                nc.scalar.copy(out=grouped[:, :SCALAR_SLOTS, :], in_=src[:, :SCALAR_SLOTS, :])
-                nc.vector.tensor_copy(out=grouped[:, SCALAR_SLOTS:, :], in_=src[:, SCALAR_SLOTS:, :])
+                cut = SCALAR_SLOTS // PACK
+                nc.scalar.copy(out=dst[:, :cut], in_=src[:, :cut])
+                nc.vector.tensor_copy(out=dst[:, cut:], in_=src[:, cut:])
             hs_codes, hs_scales = quantise("hs%d" % h, grouped[:].rearrange("p i t -> p (i t)"), HALF)
             product(grad[:, halves[h]], gout_codes[:], gout_scales[:], hs_codes[:], hs_scales[:])
 

@@ -82,13 +82,13 @@ def tile_attend_blrgated_asked_kernel(
 
         tokens = tile("tokens", [P, I // 16], U16)
         gates = tile("gates", [P, I // 16], U16)
-        nc.sync.dma_start(out=tokens[:], in_=offs)
         q_raw = load_rows("q_raw", query)
+        nc.sync.dma_start(out=tokens[:], in_=offs)
         q2_raw = load_rows("q2_raw", query2)
         load_scales(nc.sync, key_plane, keys_scales, 0)
         key_pool = load_words("key_pool", keys_words)
         q_grouped = interleave_on_scalar("q_grouped", q_raw)
-        load_scales(nc.sync, tab_plane, tab_scales, TAB_PLANE)
+        load_scales(nc.gpsimd, tab_plane, tab_scales, TAB_PLANE)
         w_raw = load_rows("w_raw", w1)
         nc.sync.dma_start(out=gates[:], in_=offs2)
         hsc_sb = tile("hsc_sb", [P, PACK], F32)
@@ -133,14 +133,14 @@ def tile_attend_blrgated_asked_kernel(
         sig2 = tile("sig2", [P, I], F32, tag="neg_score")
         nc.scalar.activation(out=sig2[:], in_=score2[:], func=ACT.Sigmoid)
 
-        tab_sc = tile("tab_sc", [P, I], U8)
-        nc.vector.tensor_copy(out=tab_sc[:], in_=tab_plane[:].indirect(tokens[:]))
         w_grouped = tile("w_grouped", [P, PACK, P, PACK], BF16)
         nc.vector.tensor_copy(
             out=w_grouped[:].rearrange("p t m j -> p m j t"),
             in_=w_raw[:].rearrange("p j (m t) -> p m j t", t=PACK),
         )
         w_codes, w_scales = quantise("w", w_grouped[:].rearrange("p t m j -> p (t m j)"), R)
+        tab_sc = tile("tab_sc", [P, I], U8, tag="w_grouped")
+        nc.vector.tensor_copy(out=tab_sc[:], in_=tab_plane[:].indirect(tokens[:]))
         tab_codes = tile("tab_codes", [P, I], U32)
         nc.vector.tensor_copy(out=tab_codes[:], in_=tab_pool[:].bitcast(U32).indirect(tokens[:]))
         hidden = []

from contextlib import ExitStack

import concourse.mybir as mybir

D, K, R, T, I, Q, U = 512, 512, 512, 2048, 512, 128, 1024
FLOPS = 2 * D * Q * I * 2 + 2 * K * R * I + 2 * R * Q * I

F32 = mybir.dt.float32
BF16 = mybir.dt.bfloat16
I32 = mybir.dt.int32
U32 = mybir.dt.uint32
U16 = mybir.dt.uint16
U8 = mybir.dt.uint8
FP8X4 = mybir.dt.float8_e4m3fn_x4
ALU = mybir.AluOpType
ACT = mybir.ActivationFunctionType
AXIS = mybir.AxisListType

P = 128
PACK = 4
HALF = I // 2
TAB_PLANE = 4
SCALAR_SLOTS = 128
OUT_EDGES = (0, 256, 768, 1280, 1792, 2048)


def tile_attend_blrgated_asked_kernel(
    tc, query, query2, keys_words, keys_scales, tab_words, tab_scales, w1, gtab, gout, hsc, old, offs2, offs, out
):
    nc = tc.nc
    with ExitStack() as ctx:
        sb = ctx.enter_context(tc.tile_pool(name="sb", bufs=1))
        ps = ctx.enter_context(tc.psum_pool(name="ps", bufs=1))

        def tile(name, shape, dtype, tag=None):
            return sb.tile(shape, dtype, name=name, tag=tag or name, align_bytes=64)

        def bank(name, width=I):
            return ps.tile([P, width], F32, name=name)

        def load_rows(name, src):
            raw = tile(name, [P, PACK, src.shape[1]], F32)
            nc.sync.dma_start(out=raw[:], in_=src.rearrange("(p j) w -> p j w", j=PACK))
            return raw

        def load_words(name, src):
            pool_words = tile(name, [P, T], I32)
            nc.sync.dma_start(out=pool_words[:], in_=src[0].rearrange("p n t -> p (n t)").bitcast(I32))
            return pool_words

        def load_scales(queue, plane, src, first):
            rows = src[0].rearrange("(g r) c -> r g c", r=PACK)
            for r in range(PACK):
                queue.dma_start(out=plane[first + r : P : 32, :].bitcast(I32), in_=rows[r].bitcast(I32))

        def quantise(name, grouped, width):
            codes = tile(name + "_codes", [P, width], U32)
            scales = tile(name + "_scales", [P, width], U8)
            nc.vector.quantize_mx(out=codes[:].bitcast(FP8X4), scales=scales[:], in_=grouped)
            return codes, scales

        def interleave_on_scalar(name, raw):
            grouped = tile(name, [P, Q, PACK], BF16)
            nc.scalar.copy(
                out=grouped[:].rearrange("p (c i) j -> p c j i", i=PACK),
                in_=raw[:].rearrange("p j (c i) -> p c j i", i=PACK),
            )
            return grouped[:].rearrange("p w j -> p (w j)")

        def product(acc, lhs, lhs_scale, rhs, rhs_scale):
            nc.tensor.matmul_mx(
                out=acc, lhsT=lhs.bitcast(FP8X4), lhsT_scale=lhs_scale,
                rhs=rhs.bitcast(FP8X4), rhs_scale=rhs_scale, start=True, stop=True,
            )

        key_plane = tile("key_plane", [P, T], U8)
        tab_plane = tile("tab_plane", [P, T], U8)
        spread = tile("spread", [P, T], F32)
        nc.vector.memset(key_plane[:].bitcast(I32), 0)
        nc.vector.memset(tab_plane[:].bitcast(I32), 0)
        nc.vector.memset(spread[:], 0.0)

        tokens = tile("tokens", [P, I // 16], U16)
        gates = tile("gates", [P, I // 16], U16)
        q_raw = load_rows("q_raw", query)
        nc.sync.dma_start(out=tokens[:], in_=offs)
        q2_raw = load_rows("q2_raw", query2)
        load_scales(nc.sync, key_plane, keys_scales, 0)
        key_pool = load_words("key_pool", keys_words)
        q_grouped = interleave_on_scalar("q_grouped", q_raw)
        load_scales(nc.gpsimd, tab_plane, tab_scales, TAB_PLANE)
        w_raw = load_rows("w_raw", w1)
        nc.sync.dma_start(out=gates[:], in_=offs2)
        hsc_sb = tile("hsc_sb", [P, PACK], F32)
        gate_rows = gtab.rearrange("(p j) u -> j p u", j=PACK)
        gate_pool = []
        for j in range(PACK):
            gate_pool.append(tile("gate_pool%d" % j, [P, U], F32))
            nc.sync.dma_start(out=gate_pool[j][:], in_=gate_rows[j])
            if j == 0:
                tab_pool = load_words("tab_pool", tab_words)
            if j == 1:
                nc.sync.dma_start(out=hsc_sb[:], in_=hsc.rearrange("(p j) o -> p (j o)", j=PACK))
        gout_raw = load_rows("gout_raw", gout)
        old_sb = tile("old_sb", [P, T], F32)
        nc.sync.dma_start(out=old_sb[:], in_=old)

        key_scales = tile("key_scales", [P, I], U8)
        nc.vector.tensor_copy(out=key_scales[:], in_=key_plane[:].indirect(tokens[:]))
        q_codes, q_scales = quantise("q", q_grouped, Q)
        halves = [slice(0, HALF), slice(HALF, I)]
        q2_codes, q2_scales = quantise("q2", interleave_on_scalar("q2_grouped", q2_raw), Q)
        key_codes = tile("key_codes", [P, I], U32)
        score = [bank("score%d" % h, HALF) for h in range(2)]
        for h in range(2):
            nc.vector.tensor_copy(
                out=key_codes[:, halves[h]], in_=key_pool[:].bitcast(U32).indirect(tokens[:, h * 16 : (h + 1) * 16])
            )
            product(score[h][:], q_codes[:], q_scales[:], key_codes[:, halves[h]], key_scales[:, halves[h]])
        score2 = bank("score2")
        product(score2[:], q2_codes[:], q2_scales[:], key_codes[:], key_scales[:])
        neg_max_first = tile("neg_max_first", [P, 1], F32)
        nc.vector.tensor_reduce(out=neg_max_first[:], in_=score[0][:], axis=AXIS.X, op=ALU.max, negate=True)
        neg_max = tile("neg_max", [P, 1], F32)
        neg_score = tile("neg_score", [P, HALF], F32)
        nc.vector.tensor_scalar(
            out=neg_score[:], in0=score[1][:], scalar1=-1.0, scalar2=neg_max_first[:], op0=ALU.mult, op1=ALU.min,
            accum_out=neg_max[:],
        )
        expd = tile("expd", [P, I], F32)
        nc.scalar.activation(out=expd[:, halves[0]], in_=score[0][:], func=ACT.Exp, bias=neg_max[:])
        nc.scalar.activation(out=expd[:, halves[1]], in_=neg_score[:], func=ACT.Exp, bias=neg_max[:], scale=-1.0)
        sig2 = tile("sig2", [P, I], F32, tag="neg_score")
        nc.scalar.activation(out=sig2[:], in_=score2[:], func=ACT.Sigmoid)

        w_grouped = tile("w_grouped", [P, PACK, P, PACK], BF16)
        nc.vector.tensor_copy(
            out=w_grouped[:].rearrange("p t m j -> p m j t"),
            in_=w_raw[:].rearrange("p j (m t) -> p m j t", t=PACK),
        )
        w_codes, w_scales = quantise("w", w_grouped[:].rearrange("p t m j -> p (t m j)"), R)
        tab_sc = tile("tab_sc", [P, I], U8, tag="w_grouped")
        nc.vector.tensor_copy(out=tab_sc[:], in_=tab_plane[:].indirect(tokens[:]))
        tab_codes = tile("tab_codes", [P, I], U32)
        nc.vector.tensor_copy(out=tab_codes[:], in_=tab_pool[:].bitcast(U32).indirect(tokens[:]))
        hidden = []
        for t in range(PACK):
            hidden.append(bank("hidden%d" % t))
            cols = slice(t * P, (t + 1) * P)
            product(hidden[t][:], w_codes[:, cols], w_scales[:, cols], tab_codes[:], tab_sc[TAB_PLANE:P, :])

        weights = tile("weights", [P, I], F32, tag="tab_pool")
        total = tile("total", [P, 1], F32)
        nc.vector.scalar_tensor_tensor(
            out=weights[:], in0=expd[:], scalar=1.0, in1=sig2[:], op0=ALU.mult, op1=ALU.mult, accum_out=total[:]
        )
        inv_total = tile("inv_total", [P, 1], F32)
        nc.vector.reciprocal(out=inv_total[:], in_=total[:])
        up = tile("up", [P, 1], F32)
        nc.vector.tensor_scalar(out=up[:], in0=inv_total[:], scalar1=512.0, scalar2=None, op0=ALU.mult)
        down = tile("down", [P, 1], F32)
        nc.vector.tensor_scalar(out=down[:], in0=inv_total[:], scalar1=-1.0, scalar2=None, op0=ALU.mult)

        planes = tile("planes", [P, PACK, I], BF16)
        for t in range(PACK):
            if t < PACK - 1:
                gate = tile("gate%d" % t, [P, I], F32)
                nc.scalar.activation(out=gate[:], in_=gate_pool[t][:].indirect(gates[:]), func=ACT.Sigmoid)
                pieces = [(slice(0, I), gate[:])]
            else:
                pieces = []
                for h in range(2):
                    gate = tile("gate_last%d" % h, [P, HALF], F32)
                    nc.scalar.activation(
                        out=gate[:], in_=gate_pool[t][:].indirect(gates[:, h * 16 : (h + 1) * 16]), func=ACT.Sigmoid
                    )
                    pieces.append((halves[h], gate[:]))
            for slots, piece in pieces:
                nc.vector.scalar_tensor_tensor(
                    out=planes[:, t, slots], in0=hidden[t][:, slots], scalar=hsc_sb[:, t : t + 1], in1=piece,
                    op0=ALU.mult, op1=ALU.mult,
                )
        gout_codes, gout_scales = quantise("gout", interleave_on_scalar("gout_grouped", gout_raw), Q)

        grad = bank("grad")
        for h in range(2):
            grouped = tile("hs_grouped%d" % h, [P, HALF, PACK], BF16)
            src = planes[:, :, halves[h]].rearrange("p t (c i) -> p c t i", i=PACK)
            dst = grouped[:].rearrange("p (c i) t -> p c t i", i=PACK)
            if h == 0:
                nc.vector.tensor_copy(out=dst, in_=src)
            else:
                cut = SCALAR_SLOTS // PACK
                nc.scalar.copy(out=dst[:, :cut], in_=src[:, :cut])
                nc.vector.tensor_copy(out=dst[:, cut:], in_=src[:, cut:])
            hs_codes, hs_scales = quantise("hs%d" % h, grouped[:].rearrange("p i t -> p (i t)"), HALF)
            product(grad[:, halves[h]], gout_codes[:], gout_scales[:], hs_codes[:], hs_scales[:])

        direct = tile("direct", [P, I], F32)
        direct_sum = tile("direct_sum", [P, 1], F32)
        nc.vector.scalar_tensor_tensor(
            out=direct[:], in0=grad[:], scalar=up[:], in1=weights[:], op0=ALU.mult, op1=ALU.mult,
            accum_out=direct_sum[:],
        )
        through_sum = tile("through_sum", [P, I], F32)
        nc.vector.tensor_scalar(
            out=through_sum[:], in0=weights[:], scalar1=direct_sum[:], scalar2=down[:], op0=ALU.mult, op1=ALU.mult
        )
        nc.vector.tensor_tensor(out=spread[:].indirect(tokens[:]), in0=direct[:], in1=through_sum[:], op=ALU.add)

        for c in range(len(OUT_EDGES) - 1):
            cols = slice(OUT_EDGES[c], OUT_EDGES[c + 1])
            result = tile("result%d" % c, [P, cols.stop - cols.start], F32)
            nc.vector.tensor_tensor(out=result[:], in0=spread[:, cols], in1=old_sb[:, cols], op=ALU.add)
            queue = nc.sync if c % 2 == 0 else nc.scalar
            queue.dma_start(out=out[:, cols], in_=result[:])
